import numpy as np
import ml_dtypes


def mxq(x, axis, fmt="e4m3"):
    dtype, down = {"e4m3": (ml_dtypes.float8_e4m3fn, 7), "e5m2": (ml_dtypes.float8_e5m2, 14)}[fmt]
    v = np.moveaxis(np.asarray(x, np.float32).astype(ml_dtypes.bfloat16).astype(np.float64), axis, -1)
    blocks = v.reshape(v.shape[:-1] + (-1, 32))
    amax = np.abs(blocks).max(-1, keepdims=True)
    byte = np.maximum(np.where(amax > 0, np.frexp(amax)[1] - 1 + 127, 0) - down, 1)
    scale = np.exp2(byte - 127.0)
    codes = (blocks / scale).astype(np.float32).astype(dtype).astype(np.float64)
    return np.moveaxis((codes * scale).reshape(v.shape), -1, axis)


WIDE = False


def mx_kscale(k):
    if not WIDE:
        return np.ones(k)
    levels = np.array([10, -10, 5, -5, 0])
    if k % 512:
        return np.exp2(np.random.permutation(np.resize(levels, k // 32))).repeat(32)
    a = np.empty((k // 512, 16))
    for p in range(k // 512):
        a[p, :8] = np.random.permutation(np.resize(levels, 8))
        for g in range(8):
            far = levels[np.abs(levels - a[p, g]) >= 10]
            a[p, g + 8] = far[np.random.randint(len(far))]
    return np.exp2(a.ravel()).repeat(32)


def f64(x):
    return np.asarray(x).astype(np.float64)


def striped(idx):
    return np.tile(idx.reshape(-1, 16).T, (8, 1)).astype(np.uint16)


def unstriped(offs):
    return offs[:16].T.reshape(-1).astype(np.int64)


def striped8(idx):
    return np.concatenate([x.reshape(-1, 16).T for x in idx]).astype(np.uint16)


def runs(offs, k):
    lists = np.stack([offs[16 * r : 16 * r + 16].T.reshape(-1) for r in range(8)]).astype(np.int64)
    return lists[np.arange(k) % 512 // 64]


def pack_weight(w):
    k, n = w.shape
    w = f64(np.asarray(w, np.float32).astype(ml_dtypes.bfloat16)).reshape(k // 32, 32, n)
    amax = np.abs(w).max(1)
    byte = np.clip(np.where(amax > 0, np.frexp(amax)[1] - 1 + 127 - 7, 1), 1, 254)
    scaled = (w * np.exp2(127.0 - byte)[:, None, :]).reshape(k, n).astype(np.float32)
    words = np.ascontiguousarray(scaled.reshape(k // 512, 128, 4, n).transpose(0, 1, 3, 2)).astype(ml_dtypes.float8_e4m3fn).view(np.uint8)
    return words, np.ascontiguousarray(byte.astype(np.uint8).reshape(k // 512, 16, n))


def unpack_weight(words, scales):
    g, p, n, _ = words.shape
    vals = np.ascontiguousarray(words).view(ml_dtypes.float8_e4m3fn).astype(np.float64) * np.repeat(np.exp2(scales.astype(np.float64) - 127.0), 8, axis=1)[..., None]
    return vals.transpose(0, 1, 3, 2).reshape(g * 512, n)


K, T, S, N, H, U = 512, 2048, 512, 512, 512, 1024


def setup_inputs():
    n = np.random.standard_normal
    s = mx_kscale(K)[:, None]
    u = mx_kscale(H)
    packed_xT = pack_weight(n((K, T)) * s)
    ang = 3 * n((H, U))
    return {
        "x_words": packed_xT[0],
        "x_scales": packed_xT[1],
        "w1": (n((K, H)) / np.sqrt(K) / s * u).astype(np.float32),
        "w2": (n((K, H)) / np.sqrt(K) / s * u).astype(np.float32),
        "ct": np.cos(ang).astype(np.float32),
        "st": np.sin(ang).astype(np.float32),
        "w3": (n((H, N)) / np.sqrt(2 * H) / u[:, None]).astype(np.float32),
        "w4": (n((H, N)) / np.sqrt(2 * H) / u[:, None]).astype(np.float32),
        "offs": striped(np.random.permutation(T)[:S]),
        "pos": striped8(np.random.randint(0, U, (8, S))),
    }


def reference(x_words, x_scales, w1, w2, ct, st, w3, w4, offs, pos):
    xq = unpack_weight(x_words, x_scales)[:, unstriped(offs)]
    y = mxq(f64(w1), 0, "e4m3").T @ xq
    c = f64(ct)[np.arange(H)[:, None], runs(pos, H)]
    e = mxq(f64(w2), 0, "e4m3").T @ xq
    q = f64(st)[np.arange(H)[:, None], runs(pos, H)]
    z = y * c - (e * q)
    z2 = y * q + e * c
    return mxq(f64(w3), 0, "e4m3").T @ mxq(z, 0, "e4m3") + mxq(f64(w4), 0, "e4m3").T @ mxq(z2, 0, "e4m3")

@@ -1,0 +1,226 @@
+from contextlib import ExitStack
+
+import concourse.mybir as mybir
+
+F32 = mybir.dt.float32
+BF16 = mybir.dt.bfloat16
+I32 = mybir.dt.int32
+U32 = mybir.dt.uint32
+U16 = mybir.dt.uint16
+U8 = mybir.dt.uint8
+FP8X4 = mybir.dt.float8_e4m3fn_x4
+MULT = mybir.AluOpType.mult
+ADD = mybir.AluOpType.add
+SUB = mybir.AluOpType.subtract
+
+P = 128
+PACK = 4
+T, S, H, N, U = 2048, 512, 512, 512, 1024
+TOK = 128
+TILES = S // TOK
+FLOPS = 2 * 4 * 512 * 512 * 512
+
+
+def tile_picked_headrope_none_p_kernel(
+    tc, x_words, x_scales, w1, w2, ct, st, w3, w4, offs, pos, out
+):
+    nc = tc.nc
+    with ExitStack() as ctx:
+        keep = ctx.enter_context(tc.tile_pool(name="keep", bufs=1))
+        ring = ctx.enter_context(tc.tile_pool(name="ring", bufs=3))
+        psum_y = ctx.enter_context(tc.psum_pool(name="psum_y", bufs=4))
+        psum = ctx.enter_context(tc.psum_pool(name="psum", bufs=2))
+
+        offs_sb = keep.tile([P, S // 16], U16, name="offs_sb")
+        pos_sb = keep.tile([P, S // 16], U16, name="pos_sb")
+        nc.sync.dma_start(pos_sb[:], pos)
+        nc.sync.dma_start(offs_sb[:], offs)
+
+        xs_all = keep.tile([P, T], U8, name="xs_all", align_bytes=64)
+        nc.vector.memset(xs_all[:].bitcast(I32), 0)
+        for quad in range(4):
+            nc.scalar.dma_start(
+                xs_all[32 * quad : 32 * quad + 4, :].bitcast(I32),
+                x_scales[0, 4 * quad : 4 * quad + 4, :].bitcast(I32),
+            )
+
+        def load_plane(table, t, name):
+            plane = keep.tile([P, U], F32, name=f"{name}{t}", tag=f"{name}{t}", align_bytes=64)
+            nc.sync.dma_start(plane[:], table.rearrange("(p t) u -> p t u", t=PACK)[:, t, :])
+            return plane
+
+        def load_weight(w, name):
+            raw = keep.tile([P, PACK, H], F32, name=f"{name}_raw", tag=f"{name}_raw", align_bytes=64)
+            nc.sync.dma_start(raw[:], w.rearrange("(p j) c -> p j c", j=PACK))
+            return raw
+
+        def quantise(grouped, name):
+            codes = keep.tile([P, H], U32, name=f"{name}_codes", align_bytes=64)
+            scales = keep.tile([P, H], U8, name=f"{name}_scales", align_bytes=64)
+            nc.vector.quantize_mx(out=codes[:].bitcast(FP8X4), scales=scales[:], in_=grouped[:])
+            return codes, scales
+
+        def group_first(raw, name, shared):
+            grouped = keep.tile([P, H * PACK], BF16, name=f"{name}_bf", align_bytes=64)
+            dst = grouped[:].rearrange("p (t m j) -> p m j t", t=PACK, j=PACK)
+            src = raw[:].rearrange("p j (m t) -> p m j t", t=PACK)
+            if shared:
+                nc.scalar.copy(out=dst[:, :, :, 0:2], in_=src[:, :, :, 0:2])
+                nc.vector.tensor_copy(out=dst[:, :, :, 2:4], in_=src[:, :, :, 2:4])
+            else:
+                nc.scalar.copy(out=dst, in_=src)
+            return grouped
+
+        def group_second(raw, name):
+            grouped = keep.tile([P, N * PACK], BF16, name=f"{name}_bf", tag=f"{name}_bf", align_bytes=64)
+            nc.scalar.copy(
+                out=grouped[:].rearrange("p (c i j) -> p c j i", i=4, j=PACK),
+                in_=raw[:].rearrange("p j (c i) -> p c j i", i=4),
+            )
+            return grouped
+
+        c_planes = keep.tile([P, PACK, S], F32, name="c_planes", align_bytes=64)
+        q_planes = keep.tile([P, PACK, S], F32, name="q_planes", align_bytes=64)
+
+        def gather(dst, t, plane):
+            nc.vector.tensor_copy(dst[:, t, :], plane[:].indirect(pos_sb[:]))
+
+        ct0 = load_plane(ct, 0, "ct")
+        xw_all = keep.tile([P, T], U32, name="xw_all", align_bytes=64)
+        nc.sync.dma_start(xw_all[:].bitcast(I32), x_words[0].rearrange("p n t -> p (n t)").bitcast(I32))
+        w1_raw = load_weight(w1, "w1")
+        ct1 = load_plane(ct, 1, "ct")
+        ct2 = load_plane(ct, 2, "ct")
+        ct3 = load_plane(ct, 3, "ct")
+        w2_raw = load_weight(w2, "w2")
+        st0 = load_plane(st, 0, "st")
+        st1 = load_plane(st, 1, "st")
+        st2 = load_plane(st, 2, "st")
+        st3 = load_plane(st, 3, "st")
+        w3_raw = load_weight(w3, "w3")
+        w4_raw = load_weight(w4, "w4")
+
+        xw = keep.tile([P, S], U32, name="xw", align_bytes=64)
+        gather(c_planes, 0, ct0)
+        xs = keep.tile([P, S], U8, name="xs", tag="ct0", align_bytes=64)
+        nc.vector.tensor_copy(xs[:], xs_all[:].indirect(offs_sb[:]))
+        nc.vector.tensor_copy(xw[:], xw_all[:].indirect(offs_sb[:]))
+        w1_bf = group_first(w1_raw, "w1", True)
+        gather(c_planes, 1, ct1)
+        w1_q = quantise(w1_bf, "w1")
+        gather(c_planes, 2, ct2)
+        gather(c_planes, 3, ct3)
+        w2_bf = group_first(w2_raw, "w2", False)
+        for t, plane in enumerate((st0, st1, st2, st3)):
+            gather(q_planes, t, plane)
+        w2_q = quantise(w2_bf, "w2")
+
+        def project(bank, wq, j):
+            cols = slice(j * TOK, (j + 1) * TOK)
+            for t in range(PACK):
+                rows = slice(t * P, (t + 1) * P)
+                nc.tensor.matmul_mx(
+                    out=bank[:, t, :],
+                    lhsT=wq[0][:, rows].bitcast(FP8X4),
+                    lhsT_scale=wq[1][:, rows],
+                    rhs=xw[:, cols].bitcast(FP8X4),
+                    rhs_scale=xs[:, cols],
+                    start=True,
+                    stop=True,
+                )
+
+        def product(dst, bank, planes, j):
+            nc.vector.tensor_tensor(dst, bank[:], planes[:, :, j * TOK : (j + 1) * TOK], MULT)
+
+        y_banks = []
+        for j in range(TILES):
+            y_bank = psum_y.tile([P, PACK, TOK], F32, name="y_bank")
+            project(y_bank, w1_q, j)
+            y_banks.append(y_bank)
+        yc_early = keep.tile([P, 2, PACK, TOK], F32, name="yc_early", align_bytes=64)
+        for j in range(2):
+            product(yc_early[:, j, :, :], y_banks[j], c_planes, j)
+        late = keep.tile([P, 2, PACK, TOK], F32, name="late", tag="st3", align_bytes=64)
+
+        w3_bf = group_second(w3_raw, "w3")
+        w4_bf = group_second(w4_raw, "w4")
+
+        second = []
+
+        def by_fours(t):
+            return t.rearrange("p t (c i) -> p c t i", i=4)
+
+        def rotate(j, adder):
+            e_bank = psum.tile([P, PACK, TOK], F32, name="e_bank")
+            project(e_bank, w2_q, j)
+            z_bf = keep.tile([P, 2, TOK * PACK], BF16, name=f"z_bf{j}", tag=f"z_bf{j}", align_bytes=64)
+            if j < 2:
+                both = ring.tile([P, 2, PACK, TOK], F32, name="both", align_bytes=64)
+                eq, yq = both[:, 0, :, :], both[:, 1, :, :]
+                yc = yc_early[:, j, :, :]
+                ec = late[:, j, :, :]
+            else:
+                tags = ("w3_bf", "w4_bf") if j == 2 else ("z_bf0", "z_bf1")
+                for_z = keep.tile([P, 2, PACK, TOK], F32, name=f"for_z{j}", tag=tags[0], align_bytes=64)
+                for_z2 = keep.tile([P, 2, PACK, TOK], F32, name=f"for_z2{j}", tag=tags[1], align_bytes=64)
+                yc, eq = for_z[:, 0, :, :], for_z[:, 1, :, :]
+                ec, yq = for_z2[:, 0, :, :], for_z2[:, 1, :, :]
+            if j > 1:
+                product(yc, y_banks[j], c_planes, j)
+            product(eq, e_bank, q_planes, j)
+            product(ec, e_bank, c_planes, j)
+            product(yq, y_banks[j], q_planes, j)
+            woven = [z_bf[:, half, :].rearrange("p (c i t) -> p c t i", i=4, t=PACK) for half in range(2)]
+            adder.tensor_tensor(woven[0], by_fours(yc), by_fours(eq), SUB)
+            adder.tensor_tensor(woven[1], by_fours(yq), by_fours(ec), ADD)
+            return z_bf
+
+        def second_pass(dst, m, half, z_codes, z_scales, cols):
+            rows = slice(m * P, (m + 1) * P)
+            nc.tensor.matmul_mx(
+                out=dst,
+                lhsT=second[half][0][:, rows].bitcast(FP8X4),
+                lhsT_scale=second[half][1][:, rows],
+                rhs=z_codes[:, cols].bitcast(FP8X4),
+                rhs_scale=z_scales[:, cols],
+                start=(half == 0),
+                stop=(half == 1),
+            )
+
+        out_tiles = out.rearrange("(m p) s -> p m s", p=P)
+
+        def finish(j, z_bf):
+            z_codes = keep.tile([P, 2 * TOK], U32, name=f"z_codes{j}", tag="w4_raw" if j < 2 else "z_codes", align_bytes=64)
+            z_scales = ring.tile([P, 2 * TOK], U8, name="z_scales", align_bytes=64)
+            nc.vector.quantize_mx(out=z_codes[:].bitcast(FP8X4), scales=z_scales[:], in_=z_bf[:].rearrange("p h n -> p (h n)"))
+            o_bank = psum.tile([P, PACK, TOK], F32, name="o_bank")
+            for m in range(N // P):
+                for half in range(2):
+                    second_pass(o_bank[:, m, :], m, half, z_codes, z_scales, slice(half * TOK, (half + 1) * TOK))
+            result = ring.tile([P, PACK, TOK], F32, name="result", align_bytes=64)
+            nc.scalar.copy(out=result[:], in_=o_bank[:])
+            nc.sync.dma_start(out_tiles[:, :, j * TOK : (j + 1) * TOK], result[:])
+
+        def finish_last(j, z_bf):
+            banks = [psum_y.tile([P, TOK], F32, name="y_bank") for m in range(N // P)]
+            for half in range(2):
+                z_codes = keep.tile([P, TOK], U32, name=f"last_codes{half}", align_bytes=64)
+                z_scales = keep.tile([P, TOK], U8, name=f"last_scales{half}", align_bytes=64)
+                nc.vector.quantize_mx(out=z_codes[:].bitcast(FP8X4), scales=z_scales[:], in_=z_bf[:, half, :])
+                for m in range(N // P):
+                    second_pass(banks[m][:], m, half, z_codes, z_scales, slice(0, TOK))
+            for pair in range(2):
+                result = keep.tile([P, 2, TOK], F32, name=f"last_result{pair}", align_bytes=64)
+                nc.scalar.copy(out=result[:, 0, :], in_=banks[2 * pair][:])
+                nc.vector.tensor_copy(out=result[:, 1, :], in_=banks[2 * pair + 1][:])
+                nc.sync.dma_start(out_tiles[:, 2 * pair : 2 * pair + 2, j * TOK : (j + 1) * TOK], result[:])
+
+        z_tiles = [rotate(0, nc.gpsimd)]
+        z_tiles.append(rotate(1, nc.gpsimd))
+        second.extend([quantise(w3_bf, "w3"), quantise(w4_bf, "w4")])
+        finish(0, z_tiles[0])
+        z_tiles.append(rotate(2, nc.gpsimd))
+        finish(1, z_tiles[1])
+        z_tiles.append(rotate(3, nc.vector))
+        finish(2, z_tiles[2])
+        finish_last(3, z_tiles[3])

@@ -74,8 +74,8 @@ def tile_picked_headrope_none_p_kernel(
         def group_second(raw, name):
             grouped = keep.tile([P, N * PACK], BF16, name=f"{name}_bf", tag=f"{name}_bf", align_bytes=64)
             nc.scalar.copy(
-                out=grouped[:].rearrange("p (c i j) -> p c j i", i=4, j=PACK),
-                in_=raw[:].rearrange("p j (c i) -> p c j i", i=4),
+                out=grouped[:].rearrange("p (c i j) -> p c j i", i=2, j=PACK),
+                in_=raw[:].rearrange("p j (c i) -> p c j i", i=2),
             )
             return grouped
 
@@ -137,42 +137,31 @@ def tile_picked_headrope_none_p_kernel(
             y_bank = psum_y.tile([P, PACK, TOK], F32, name="y_bank")
             project(y_bank, w1_q, j)
             y_banks.append(y_bank)
-        yc_early = keep.tile([P, 2, PACK, TOK], F32, name="yc_early", align_bytes=64)
-        for j in range(2):
-            product(yc_early[:, j, :, :], y_banks[j], c_planes, j)
-        late = keep.tile([P, 2, PACK, TOK], F32, name="late", tag="st3", align_bytes=64)
+        yc = [keep.tile([P, PACK, TOK], F32, name=f"yc{j}", align_bytes=64) for j in range(TILES)]
+        for j in range(TILES):
+            product(yc[j][:], y_banks[j], c_planes, j)
 
         w3_bf = group_second(w3_raw, "w3")
         w4_bf = group_second(w4_raw, "w4")
 
         second = []
 
-        def by_fours(t):
-            return t.rearrange("p t (c i) -> p c t i", i=4)
+        def by_pairs(t):
+            return t.rearrange("p t (c i) -> p c t i", i=2)
 
-        def rotate(j, adder):
+        def rotate(j, slot):
             e_bank = psum.tile([P, PACK, TOK], F32, name="e_bank")
             project(e_bank, w2_q, j)
             z_bf = keep.tile([P, 2, TOK * PACK], BF16, name=f"z_bf{j}", tag=f"z_bf{j}", align_bytes=64)
-            if j < 2:
-                both = ring.tile([P, 2, PACK, TOK], F32, name="both", align_bytes=64)
-                eq, yq = both[:, 0, :, :], both[:, 1, :, :]
-                yc = yc_early[:, j, :, :]
-                ec = late[:, j, :, :]
-            else:
-                tags = ("w3_bf", "w4_bf") if j == 2 else ("z_bf0", "z_bf1")
-                for_z = keep.tile([P, 2, PACK, TOK], F32, name=f"for_z{j}", tag=tags[0], align_bytes=64)
-                for_z2 = keep.tile([P, 2, PACK, TOK], F32, name=f"for_z2{j}", tag=tags[1], align_bytes=64)
-                yc, eq = for_z[:, 0, :, :], for_z[:, 1, :, :]
-                ec, yq = for_z2[:, 0, :, :], for_z2[:, 1, :, :]
-            if j > 1:
-                product(yc, y_banks[j], c_planes, j)
+            ec = keep.tile([P, PACK, TOK], F32, name=f"ec{j}", align_bytes=64)
+            with_q = keep.tile([P, 2, PACK, TOK], F32, name=f"with_q{j}", tag=slot, align_bytes=64)
+            eq, yq = with_q[:, 0, :, :], with_q[:, 1, :, :]
+            product(ec[:], e_bank, c_planes, j)
             product(eq, e_bank, q_planes, j)
-            product(ec, e_bank, c_planes, j)
             product(yq, y_banks[j], q_planes, j)
-            woven = [z_bf[:, half, :].rearrange("p (c i t) -> p c t i", i=4, t=PACK) for half in range(2)]
-            adder.tensor_tensor(woven[0], by_fours(yc), by_fours(eq), SUB)
-            adder.tensor_tensor(woven[1], by_fours(yq), by_fours(ec), ADD)
+            woven = [z_bf[:, half, :].rearrange("p (c i t) -> p c t i", i=2, t=PACK) for half in range(2)]
+            nc.vector.tensor_tensor(woven[0], by_pairs(yc[j][:]), by_pairs(eq), SUB)
+            nc.vector.tensor_tensor(woven[1], by_pairs(yq), by_pairs(ec[:]), ADD)
             return z_bf
 
         def second_pass(dst, m, half, z_codes, z_scales, cols):
@@ -190,7 +179,7 @@ def tile_picked_headrope_none_p_kernel(
         out_tiles = out.rearrange("(m p) s -> p m s", p=P)
 
         def finish(j, z_bf):
-            z_codes = keep.tile([P, 2 * TOK], U32, name=f"z_codes{j}", tag="w4_raw" if j < 2 else "z_codes", align_bytes=64)
+            z_codes = keep.tile([P, 2 * TOK], U32, name=f"z_codes{j}", tag="w4_raw" if j == 0 else f"z_codes{j}", align_bytes=64)
             z_scales = ring.tile([P, 2 * TOK], U8, name="z_scales", align_bytes=64)
             nc.vector.quantize_mx(out=z_codes[:].bitcast(FP8X4), scales=z_scales[:], in_=z_bf[:].rearrange("p h n -> p (h n)"))
             o_bank = psum.tile([P, PACK, TOK], F32, name="o_bank")
@@ -215,12 +204,9 @@ def tile_picked_headrope_none_p_kernel(
                 nc.vector.tensor_copy(out=result[:, 1, :], in_=banks[2 * pair + 1][:])
                 nc.sync.dma_start(out_tiles[:, 2 * pair : 2 * pair + 2, j * TOK : (j + 1) * TOK], result[:])
 
-        z_tiles = [rotate(0, nc.gpsimd)]
-        z_tiles.append(rotate(1, nc.gpsimd))
+        z_first = rotate(0, "with_q0")
         second.extend([quantise(w3_bf, "w3"), quantise(w4_bf, "w4")])
-        finish(0, z_tiles[0])
-        z_tiles.append(rotate(2, nc.gpsimd))
-        finish(1, z_tiles[1])
-        z_tiles.append(rotate(3, nc.vector))
-        finish(2, z_tiles[2])
-        finish_last(3, z_tiles[3])
+        finish(0, z_first)
+        finish(1, rotate(1, "w4_bf"))
+        finish(2, rotate(2, "z_bf0"))
+        finish_last(3, rotate(3, "z_bf1"))

@@ -1,6 +1,7 @@
 from contextlib import ExitStack
 
 import concourse.mybir as mybir
+from concourse.masks import make_identity
 
 F32 = mybir.dt.float32
 BF16 = mybir.dt.bfloat16
@@ -18,6 +19,7 @@ PACK = 4
 T, S, H, N, U = 2048, 512, 512, 512, 1024
 TOK = 128
 TILES = S // TOK
+TURNED = 2
 FLOPS = 2 * 4 * 512 * 512 * 512
 
 
@@ -28,21 +30,15 @@ def tile_picked_headrope_none_p_kernel(
     with ExitStack() as ctx:
         keep = ctx.enter_context(tc.tile_pool(name="keep", bufs=1))
         ring = ctx.enter_context(tc.tile_pool(name="ring", bufs=3))
-        psum_y = ctx.enter_context(tc.psum_pool(name="psum_y", bufs=4))
+        psum_one = ctx.enter_context(tc.psum_pool(name="psum_one", bufs=1))
         psum = ctx.enter_context(tc.psum_pool(name="psum", bufs=2))
+        ident = keep.tile([P, P], F32, name="ident", align_bytes=64)
+        make_identity(nc, ident[:])
 
         offs_sb = keep.tile([P, S // 16], U16, name="offs_sb")
         pos_sb = keep.tile([P, S // 16], U16, name="pos_sb")
-        nc.sync.dma_start(pos_sb[:], pos)
-        nc.sync.dma_start(offs_sb[:], offs)
-
         xs_all = keep.tile([P, T], U8, name="xs_all", align_bytes=64)
         nc.vector.memset(xs_all[:].bitcast(I32), 0)
-        for quad in range(4):
-            nc.scalar.dma_start(
-                xs_all[32 * quad : 32 * quad + 4, :].bitcast(I32),
-                x_scales[0, 4 * quad : 4 * quad + 4, :].bitcast(I32),
-            )
 
         def load_plane(table, t, name):
             plane = keep.tile([P, U], F32, name=f"{name}{t}", tag=f"{name}{t}", align_bytes=64)
@@ -71,13 +67,12 @@ def tile_picked_headrope_none_p_kernel(
                 nc.scalar.copy(out=dst, in_=src)
             return grouped
 
-        def group_second(raw, name):
-            grouped = keep.tile([P, N * PACK], BF16, name=f"{name}_bf", tag=f"{name}_bf", align_bytes=64)
+        def group_second(grouped, raw, half):
+            cols = slice(half * N // 4, (half + 1) * N // 4)
             nc.scalar.copy(
-                out=grouped[:].rearrange("p (c i j) -> p c j i", i=2, j=PACK),
-                in_=raw[:].rearrange("p j (c i) -> p c j i", i=2),
+                out=grouped[:].rearrange("p (c i j) -> p c j i", i=2, j=PACK)[:, cols, :, :],
+                in_=raw[:].rearrange("p j (c i) -> p c j i", i=2)[:, cols, :, :],
             )
-            return grouped
 
         c_planes = keep.tile([P, PACK, S], F32, name="c_planes", align_bytes=64)
         q_planes = keep.tile([P, PACK, S], F32, name="q_planes", align_bytes=64)
@@ -86,16 +81,23 @@ def tile_picked_headrope_none_p_kernel(
             nc.vector.tensor_copy(dst[:, t, :], plane[:].indirect(pos_sb[:]))
 
         ct0 = load_plane(ct, 0, "ct")
+        nc.sync.dma_start(pos_sb[:], pos)
+        nc.sync.dma_start(offs_sb[:], offs)
+        for quad in range(4):
+            nc.sync.dma_start(
+                xs_all[32 * quad : 32 * quad + 4, :].bitcast(I32),
+                x_scales[0, 4 * quad : 4 * quad + 4, :].bitcast(I32),
+            )
         xw_all = keep.tile([P, T], U32, name="xw_all", align_bytes=64)
         nc.sync.dma_start(xw_all[:].bitcast(I32), x_words[0].rearrange("p n t -> p (n t)").bitcast(I32))
-        w1_raw = load_weight(w1, "w1")
         ct1 = load_plane(ct, 1, "ct")
         ct2 = load_plane(ct, 2, "ct")
         ct3 = load_plane(ct, 3, "ct")
-        w2_raw = load_weight(w2, "w2")
         st0 = load_plane(st, 0, "st")
+        w1_raw = load_weight(w1, "w1")
         st1 = load_plane(st, 1, "st")
         st2 = load_plane(st, 2, "st")
+        w2_raw = load_weight(w2, "w2")
         st3 = load_plane(st, 3, "st")
         w3_raw = load_weight(w3, "w3")
         w4_raw = load_weight(w4, "w4")
@@ -105,15 +107,6 @@ def tile_picked_headrope_none_p_kernel(
         xs = keep.tile([P, S], U8, name="xs", tag="ct0", align_bytes=64)
         nc.vector.tensor_copy(xs[:], xs_all[:].indirect(offs_sb[:]))
         nc.vector.tensor_copy(xw[:], xw_all[:].indirect(offs_sb[:]))
-        w1_bf = group_first(w1_raw, "w1", True)
-        gather(c_planes, 1, ct1)
-        w1_q = quantise(w1_bf, "w1")
-        gather(c_planes, 2, ct2)
-        gather(c_planes, 3, ct3)
-        w2_bf = group_first(w2_raw, "w2", False)
-        for t, plane in enumerate((st0, st1, st2, st3)):
-            gather(q_planes, t, plane)
-        w2_q = quantise(w2_bf, "w2")
 
         def project(bank, wq, j):
             cols = slice(j * TOK, (j + 1) * TOK)
@@ -132,36 +125,105 @@ def tile_picked_headrope_none_p_kernel(
         def product(dst, bank, planes, j):
             nc.vector.tensor_tensor(dst, bank[:], planes[:, :, j * TOK : (j + 1) * TOK], MULT)
 
-        y_banks = []
-        for j in range(TILES):
-            y_bank = psum_y.tile([P, PACK, TOK], F32, name="y_bank")
-            project(y_bank, w1_q, j)
-            y_banks.append(y_bank)
-        yc = [keep.tile([P, PACK, TOK], F32, name=f"yc{j}", align_bytes=64) for j in range(TILES)]
-        for j in range(TILES):
-            product(yc[j][:], y_banks[j], c_planes, j)
+        def project_turned(bank, wq, j):
+            cols = slice(j * TOK, (j + 1) * TOK)
+            nc.tensor.matmul_mx(
+                out=bank[:].rearrange("p t m -> p (t m)"),
+                lhsT=xw[:, cols].bitcast(FP8X4),
+                lhsT_scale=xs[:, cols],
+                rhs=wq[0][:].bitcast(FP8X4),
+                rhs_scale=wq[1][:],
+                start=True,
+                stop=True,
+            )
 
-        w3_bf = group_second(w3_raw, "w3")
-        w4_bf = group_second(w4_raw, "w4")
+        def turn_table(turned, planes, j):
+            bank = psum.tile([P, PACK, P], F32, name="turn_bank")
+            for t in range(PACK):
+                nc.tensor.transpose(bank[:, t, :], planes[:, t, j * TOK : (j + 1) * TOK], ident[:])
+            nc.scalar.copy(out=turned, in_=bank[:])
 
-        second = []
+        def flat(ap):
+            return ap.rearrange("p a b -> p (a b)")
+
+        def turn_sum(dst, left, right):
+            bank = psum.tile([P, PACK, TOK], F32, name="turn_bank")
+            for t in range(PACK):
+                nc.tensor.matmul(bank[:, t, :], left[:, t, :], ident[:], start=True, stop=False, is_transpose=True)
+                nc.tensor.matmul(bank[:, t, :], right[:, t, :], ident[:], start=False, stop=True, is_transpose=True)
+            nc.scalar.copy(out=dst.rearrange("p (c t) -> p c t", t=PACK), in_=bank[:].rearrange("p t c -> p c t"))
+
+        def tile_of(name, j):
+            return keep.tile([P, PACK, TOK], F32, name=f"{name}{j}", align_bytes=64)
+
+        y_plain, yc_plain = {}, {}
+        w3_bf = keep.tile([P, N * PACK], BF16, name="w3_bf", tag="w3_bf", align_bytes=64)
+        w4_bf = keep.tile([P, N * PACK], BF16, name="w4_bf", tag="w4_bf", align_bytes=64)
+        gather(c_planes, 1, ct1)
+        gather(c_planes, 2, ct2)
+        gather(c_planes, 3, ct3)
+        c_turned = keep.tile([P, TURNED, PACK, P], F32, name="c_turned", tag="c_turned", align_bytes=64)
+        for j in range(TURNED):
+            turn_table(c_turned[:, j, :, :], c_planes, j)
+        gather(q_planes, 0, st0)
+        w1_bf = group_first(w1_raw, "w1", True)
+        gather(q_planes, 1, st1)
+        gather(q_planes, 2, st2)
+        w1_q = quantise(w1_bf, "w1")
+        w2_bf = group_first(w2_raw, "w2", False)
+        gather(q_planes, 3, st3)
+        q_turned = keep.tile([P, TURNED, PACK, P], F32, name="q_turned", tag="q_turned", align_bytes=64)
+        for j in range(TURNED):
+            turn_table(q_turned[:, j, :, :], q_planes, j)
+        w2_q = quantise(w2_bf, "w2")
+        for j in range(TURNED, TILES):
+            y_plain[j] = psum_one.tile([P, PACK, TOK], F32, name=f"y_plain{j}")
+            project(y_plain[j], w1_q, j)
+            yc_plain[j] = tile_of("yc", j)
+            product(yc_plain[j][:], y_plain[j], c_planes, j)
+        ec_turned = keep.tile([P, TURNED, PACK, P], F32, name="ec_turned", tag="ec_turned", align_bytes=64)
+        group_second(w3_bf, w3_raw, 0)
+        group_second(w3_bf, w3_raw, 1)
+        second = [quantise(w3_bf, "w3")]
+        group_second(w4_bf, w4_raw, 0)
+
+        def rotate_turned(j):
+            y_bank = psum.tile([P, PACK, P], F32, name="y_bank")
+            e_bank = psum.tile([P, PACK, P], F32, name="e_bank")
+            project_turned(y_bank, w1_q, j)
+            project_turned(e_bank, w2_q, j)
+            yc, minus_eq, yq = tile_of("yc", j), tile_of("minus_eq", j), tile_of("yq", j)
+            ec = ec_turned[:, j, :, :]
+            nc.vector.tensor_tensor(yc[:], y_bank[:], c_turned[:, j, :, :], MULT)
+            nc.vector.scalar_tensor_tensor(flat(minus_eq[:]), flat(e_bank[:]), -1.0, flat(q_turned[:, j, :, :]), MULT, MULT)
+            nc.vector.tensor_tensor(ec, e_bank[:], c_turned[:, j, :, :], MULT)
+            nc.vector.tensor_tensor(yq[:], y_bank[:], q_turned[:, j, :, :], MULT)
+            return yc[:], minus_eq[:], yq[:], ec
+
+        def sums_turned(j, parts):
+            z_bf = keep.tile([P, 2, TOK * PACK], BF16, name=f"z_bf{j}", tag=f"z_bf{j}", align_bytes=64)
+            turn_sum(z_bf[:, 0, :], parts[0], parts[1])
+            turn_sum(z_bf[:, 1, :], parts[2], parts[3])
+            return z_bf
 
         def by_pairs(t):
             return t.rearrange("p t (c i) -> p c t i", i=2)
 
-        def rotate(j, slot):
+        def project_e(j):
             e_bank = psum.tile([P, PACK, TOK], F32, name="e_bank")
             project(e_bank, w2_q, j)
+            return e_bank
+
+        def rotate_plain(j, e_bank, slot):
             z_bf = keep.tile([P, 2, TOK * PACK], BF16, name=f"z_bf{j}", tag=f"z_bf{j}", align_bytes=64)
-            ec = keep.tile([P, PACK, TOK], F32, name=f"ec{j}", align_bytes=64)
-            with_q = keep.tile([P, 2, PACK, TOK], F32, name=f"with_q{j}", tag=slot, align_bytes=64)
-            eq, yq = with_q[:, 0, :, :], with_q[:, 1, :, :]
-            product(ec[:], e_bank, c_planes, j)
+            held = keep.tile([P, 3, PACK, TOK], F32, name=f"held{j}", tag=slot, align_bytes=64)
+            eq, ec, yq = held[:, 0, :, :], held[:, 1, :, :], held[:, 2, :, :]
             product(eq, e_bank, q_planes, j)
-            product(yq, y_banks[j], q_planes, j)
+            product(ec, e_bank, c_planes, j)
+            product(yq, y_plain[j], q_planes, j)
             woven = [z_bf[:, half, :].rearrange("p (c i t) -> p c t i", i=2, t=PACK) for half in range(2)]
-            nc.vector.tensor_tensor(woven[0], by_pairs(yc[j][:]), by_pairs(eq), SUB)
-            nc.vector.tensor_tensor(woven[1], by_pairs(yq), by_pairs(ec[:]), ADD)
+            nc.vector.tensor_tensor(woven[0], by_pairs(yc_plain[j][:]), by_pairs(eq), SUB)
+            nc.vector.tensor_tensor(woven[1], by_pairs(yq), by_pairs(ec), ADD)
             return z_bf
 
         def second_pass(dst, m, half, z_codes, z_scales, cols):
@@ -179,10 +241,10 @@ def tile_picked_headrope_none_p_kernel(
         out_tiles = out.rearrange("(m p) s -> p m s", p=P)
 
         def finish(j, z_bf):
-            z_codes = keep.tile([P, 2 * TOK], U32, name=f"z_codes{j}", tag="w4_raw" if j == 0 else f"z_codes{j}", align_bytes=64)
+            z_codes = keep.tile([P, 2 * TOK], U32, name=f"z_codes{j}", align_bytes=64)
             z_scales = ring.tile([P, 2 * TOK], U8, name="z_scales", align_bytes=64)
             nc.vector.quantize_mx(out=z_codes[:].bitcast(FP8X4), scales=z_scales[:], in_=z_bf[:].rearrange("p h n -> p (h n)"))
-            o_bank = psum.tile([P, PACK, TOK], F32, name="o_bank")
+            o_bank = psum.tile([P, PACK, TOK], F32, name="y_bank")
             for m in range(N // P):
                 for half in range(2):
                     second_pass(o_bank[:, m, :], m, half, z_codes, z_scales, slice(half * TOK, (half + 1) * TOK))
@@ -190,23 +252,43 @@ def tile_picked_headrope_none_p_kernel(
             nc.scalar.copy(out=result[:], in_=o_bank[:])
             nc.sync.dma_start(out_tiles[:, :, j * TOK : (j + 1) * TOK], result[:])
 
-        def finish_last(j, z_bf):
-            banks = [psum_y.tile([P, TOK], F32, name="y_bank") for m in range(N // P)]
-            for half in range(2):
+        def rotate_and_finish_last(j, e_bank, slot):
+            z_bf = keep.tile([P, 2, TOK * PACK], BF16, name=f"z_bf{j}", align_bytes=64)
+            held = keep.tile([P, 3, PACK, TOK], F32, name=f"held{j}", tag=slot, align_bytes=64)
+            eq, ec, yq = held[:, 0, :, :], held[:, 1, :, :], held[:, 2, :, :]
+            woven = [z_bf[:, half, :].rearrange("p (c i t) -> p c t i", i=2, t=PACK) for half in range(2)]
+            banks = [psum.tile([P, TOK], F32, name=("turn_bank", "e_bank")[m // 2]) for m in range(N // P)]
+
+            def half_product(half):
                 z_codes = keep.tile([P, TOK], U32, name=f"last_codes{half}", align_bytes=64)
                 z_scales = keep.tile([P, TOK], U8, name=f"last_scales{half}", align_bytes=64)
                 nc.vector.quantize_mx(out=z_codes[:].bitcast(FP8X4), scales=z_scales[:], in_=z_bf[:, half, :])
                 for m in range(N // P):
                     second_pass(banks[m][:], m, half, z_codes, z_scales, slice(0, TOK))
-            for pair in range(2):
-                result = keep.tile([P, 2, TOK], F32, name=f"last_result{pair}", align_bytes=64)
-                nc.scalar.copy(out=result[:, 0, :], in_=banks[2 * pair][:])
-                nc.vector.tensor_copy(out=result[:, 1, :], in_=banks[2 * pair + 1][:])
-                nc.sync.dma_start(out_tiles[:, 2 * pair : 2 * pair + 2, j * TOK : (j + 1) * TOK], result[:])
 
-        z_first = rotate(0, "with_q0")
-        second.extend([quantise(w3_bf, "w3"), quantise(w4_bf, "w4")])
-        finish(0, z_first)
-        finish(1, rotate(1, "w4_bf"))
-        finish(2, rotate(2, "z_bf0"))
-        finish_last(3, rotate(3, "z_bf1"))
+            product(eq, e_bank, q_planes, j)
+            product(yq, y_plain[j], q_planes, j)
+            nc.vector.tensor_tensor(woven[0], by_pairs(yc_plain[j][:]), by_pairs(eq), SUB)
+            product(ec, e_bank, c_planes, j)
+            half_product(0)
+            nc.vector.tensor_tensor(woven[1], by_pairs(yq), by_pairs(ec), ADD)
+            half_product(1)
+            for pair, (copy, queue) in enumerate(((nc.scalar.copy, nc.scalar), (nc.vector.tensor_copy, nc.sync))):
+                result = keep.tile([P, 2, TOK], F32, name=f"last_result{pair}", align_bytes=64)
+                for m in range(2):
+                    copy(out=result[:, m, :], in_=banks[2 * pair + m][:])
+                queue.dma_start(out_tiles[:, 2 * pair : 2 * pair + 2, j * TOK : (j + 1) * TOK], result[:])
+
+        p0 = rotate_turned(0)
+        p1 = rotate_turned(1)
+        e2 = project_e(2)
+        e3 = project_e(3)
+        z0 = sums_turned(0, p0)
+        group_second(w4_bf, w4_raw, 1)
+        z1 = sums_turned(1, p1)
+        z2 = rotate_plain(2, e2, "held2")
+        second.append(quantise(w4_bf, "w4"))
+        finish(0, z0)
+        finish(1, z1)
+        finish(2, z2)
+        rotate_and_finish_last(3, e3, "w4_bf")

@@ -16,11 +16,11 @@ SUB = mybir.AluOpType.subtract
 
 P = 128
 PACK = 4
-T, S, H, N, U = 2048, 512, 512, 512, 1024
+TOKENS, PICKED, WIDTH, POSITIONS = 2048, 512, 512, 1024
 TOK = 128
-TILES = S // TOK
+TILES = PICKED // TOK
 TURNED = 2
-FLOPS = 2 * 4 * 512 * 512 * 512
+FLOPS = 4 * 2 * 512 * 512 * 512
 
 
 def tile_picked_headrope_none_p_kernel(
@@ -29,58 +29,29 @@ def tile_picked_headrope_none_p_kernel(
     nc = tc.nc
     with ExitStack() as ctx:
         keep = ctx.enter_context(tc.tile_pool(name="keep", bufs=1))
-        ring = ctx.enter_context(tc.tile_pool(name="ring", bufs=3))
-        psum_one = ctx.enter_context(tc.psum_pool(name="psum_one", bufs=1))
+        ring = ctx.enter_context(tc.tile_pool(name="ring", bufs=TILES - 1))
+        psum_held = ctx.enter_context(tc.psum_pool(name="psum_held", bufs=1))
         psum = ctx.enter_context(tc.psum_pool(name="psum", bufs=2))
+
         ident = keep.tile([P, P], F32, name="ident", align_bytes=64)
         make_identity(nc, ident[:])
 
-        offs_sb = keep.tile([P, S // 16], U16, name="offs_sb")
-        pos_sb = keep.tile([P, S // 16], U16, name="pos_sb")
-        xs_all = keep.tile([P, T], U8, name="xs_all", align_bytes=64)
+        offs_sb = keep.tile([P, PICKED // 16], U16, name="offs_sb")
+        pos_sb = keep.tile([P, PICKED // 16], U16, name="pos_sb")
+        xs_all = keep.tile([P, TOKENS], U8, name="xs_all", align_bytes=64)
         nc.vector.memset(xs_all[:].bitcast(I32), 0)
 
         def load_plane(table, t, name):
-            plane = keep.tile([P, U], F32, name=f"{name}{t}", tag=f"{name}{t}", align_bytes=64)
+            plane = keep.tile([P, POSITIONS], F32, name=f"{name}{t}", tag=f"{name}{t}", align_bytes=64)
             nc.sync.dma_start(plane[:], table.rearrange("(p t) u -> p t u", t=PACK)[:, t, :])
             return plane
 
         def load_weight(w, name):
-            raw = keep.tile([P, PACK, H], F32, name=f"{name}_raw", tag=f"{name}_raw", align_bytes=64)
+            raw = keep.tile([P, PACK, WIDTH], F32, name=f"{name}_raw", align_bytes=64)
             nc.sync.dma_start(raw[:], w.rearrange("(p j) c -> p j c", j=PACK))
             return raw
 
-        def quantise(grouped, name):
-            codes = keep.tile([P, H], U32, name=f"{name}_codes", align_bytes=64)
-            scales = keep.tile([P, H], U8, name=f"{name}_scales", align_bytes=64)
-            nc.vector.quantize_mx(out=codes[:].bitcast(FP8X4), scales=scales[:], in_=grouped[:])
-            return codes, scales
-
-        def group_first(raw, name, shared):
-            grouped = keep.tile([P, H * PACK], BF16, name=f"{name}_bf", align_bytes=64)
-            dst = grouped[:].rearrange("p (t m j) -> p m j t", t=PACK, j=PACK)
-            src = raw[:].rearrange("p j (m t) -> p m j t", t=PACK)
-            if shared:
-                nc.scalar.copy(out=dst[:, :, :, 0:2], in_=src[:, :, :, 0:2])
-                nc.vector.tensor_copy(out=dst[:, :, :, 2:4], in_=src[:, :, :, 2:4])
-            else:
-                nc.scalar.copy(out=dst, in_=src)
-            return grouped
-
-        def group_second(grouped, raw, half):
-            cols = slice(half * N // 4, (half + 1) * N // 4)
-            nc.scalar.copy(
-                out=grouped[:].rearrange("p (c i j) -> p c j i", i=2, j=PACK)[:, cols, :, :],
-                in_=raw[:].rearrange("p j (c i) -> p c j i", i=2)[:, cols, :, :],
-            )
-
-        c_planes = keep.tile([P, PACK, S], F32, name="c_planes", align_bytes=64)
-        q_planes = keep.tile([P, PACK, S], F32, name="q_planes", align_bytes=64)
-
-        def gather(dst, t, plane):
-            nc.vector.tensor_copy(dst[:, t, :], plane[:].indirect(pos_sb[:]))
-
-        ct0 = load_plane(ct, 0, "ct")
+        ct_planes = [load_plane(ct, 0, "ct")]
         nc.sync.dma_start(pos_sb[:], pos)
         nc.sync.dma_start(offs_sb[:], offs)
         for quad in range(4):
@@ -88,207 +59,259 @@ def tile_picked_headrope_none_p_kernel(
                 xs_all[32 * quad : 32 * quad + 4, :].bitcast(I32),
                 x_scales[0, 4 * quad : 4 * quad + 4, :].bitcast(I32),
             )
-        xw_all = keep.tile([P, T], U32, name="xw_all", align_bytes=64)
+        xw_all = keep.tile([P, TOKENS], U32, name="xw_all", align_bytes=64)
         nc.sync.dma_start(xw_all[:].bitcast(I32), x_words[0].rearrange("p n t -> p (n t)").bitcast(I32))
-        ct1 = load_plane(ct, 1, "ct")
-        ct2 = load_plane(ct, 2, "ct")
-        ct3 = load_plane(ct, 3, "ct")
-        st0 = load_plane(st, 0, "st")
+        ct_planes.extend([load_plane(ct, t, "ct") for t in (1, 2, 3)])
+        st_planes = [load_plane(st, 0, "st")]
         w1_raw = load_weight(w1, "w1")
-        st1 = load_plane(st, 1, "st")
-        st2 = load_plane(st, 2, "st")
+        st_planes.extend([load_plane(st, t, "st") for t in (1, 2)])
         w2_raw = load_weight(w2, "w2")
-        st3 = load_plane(st, 3, "st")
+        st_planes.append(load_plane(st, 3, "st"))
         w3_raw = load_weight(w3, "w3")
         w4_raw = load_weight(w4, "w4")
 
-        xw = keep.tile([P, S], U32, name="xw", align_bytes=64)
-        gather(c_planes, 0, ct0)
-        xs = keep.tile([P, S], U8, name="xs", tag="ct0", align_bytes=64)
+        def operand_tiles(name, words):
+            codes = keep.tile([P, words], U32, name=f"{name}_codes", align_bytes=64)
+            scales = keep.tile([P, words], U8, name=f"{name}_scales", align_bytes=64)
+            return codes, scales
+
+        def quantise(grouped, name):
+            codes, scales = operand_tiles(name, grouped.shape[1] // PACK)
+            nc.vector.quantize_mx(out=codes[:].bitcast(FP8X4), scales=scales[:], in_=grouped)
+            return codes, scales
+
+        def bf16_weight(name):
+            return keep.tile([P, WIDTH * PACK], BF16, name=f"{name}_bf", tag=f"{name}_bf", align_bytes=64)
+
+        def dealt_views(grouped, raw):
+            return (
+                grouped[:].rearrange("p (t m j) -> p m j t", t=PACK, j=PACK),
+                raw[:].rearrange("p j (m t) -> p m j t", t=PACK),
+            )
+
+        def round_half(grouped, raw, half):
+            pairs = slice(half * WIDTH // 4, (half + 1) * WIDTH // 4)
+            nc.scalar.copy(
+                out=grouped[:].rearrange("p (c i j) -> p c j i", i=2, j=PACK)[:, pairs, :, :],
+                in_=raw[:].rearrange("p j (c i) -> p c j i", i=2)[:, pairs, :, :],
+            )
+
+        c_planes = keep.tile([P, PACK, PICKED], F32, name="c_planes", align_bytes=64)
+        q_planes = keep.tile([P, PACK, PICKED], F32, name="q_planes", align_bytes=64)
+
+        def gather(planes, windows, t):
+            nc.vector.tensor_copy(planes[:, t, :], windows[t][:].indirect(pos_sb[:]))
+
+        def tokens(j):
+            return slice(j * TOK, (j + 1) * TOK)
+
+        def product_tile(name):
+            return keep.tile([P, PACK, TOK], F32, name=name, align_bytes=64)
+
+        xw = keep.tile([P, PICKED], U32, name="xw", align_bytes=64)
+        gather(c_planes, ct_planes, 0)
+        xs = keep.tile([P, PICKED], U8, name="xs", tag="ct0", align_bytes=64)
         nc.vector.tensor_copy(xs[:], xs_all[:].indirect(offs_sb[:]))
         nc.vector.tensor_copy(xw[:], xw_all[:].indirect(offs_sb[:]))
 
-        def project(bank, wq, j):
-            cols = slice(j * TOK, (j + 1) * TOK)
+        def project_plain(bank, weight, j):
+            codes, scales = weight
             for t in range(PACK):
-                rows = slice(t * P, (t + 1) * P)
+                words = slice(t * P, (t + 1) * P)
                 nc.tensor.matmul_mx(
                     out=bank[:, t, :],
-                    lhsT=wq[0][:, rows].bitcast(FP8X4),
-                    lhsT_scale=wq[1][:, rows],
-                    rhs=xw[:, cols].bitcast(FP8X4),
-                    rhs_scale=xs[:, cols],
+                    lhsT=codes[:, words].bitcast(FP8X4),
+                    lhsT_scale=scales[:, words],
+                    rhs=xw[:, tokens(j)].bitcast(FP8X4),
+                    rhs_scale=xs[:, tokens(j)],
                     start=True,
                     stop=True,
                 )
 
-        def product(dst, bank, planes, j):
-            nc.vector.tensor_tensor(dst, bank[:], planes[:, :, j * TOK : (j + 1) * TOK], MULT)
-
-        def project_turned(bank, wq, j):
-            cols = slice(j * TOK, (j + 1) * TOK)
+        def project_turned(bank, weight, j):
+            codes, scales = weight
             nc.tensor.matmul_mx(
-                out=bank[:].rearrange("p t m -> p (t m)"),
-                lhsT=xw[:, cols].bitcast(FP8X4),
-                lhsT_scale=xs[:, cols],
-                rhs=wq[0][:].bitcast(FP8X4),
-                rhs_scale=wq[1][:],
+                out=bank[:].rearrange("s t m -> s (t m)"),
+                lhsT=xw[:, tokens(j)].bitcast(FP8X4),
+                lhsT_scale=xs[:, tokens(j)],
+                rhs=codes[:].bitcast(FP8X4),
+                rhs_scale=scales[:],
                 start=True,
                 stop=True,
             )
 
-        def turn_table(turned, planes, j):
-            bank = psum.tile([P, PACK, P], F32, name="turn_bank")
-            for t in range(PACK):
-                nc.tensor.transpose(bank[:, t, :], planes[:, t, j * TOK : (j + 1) * TOK], ident[:])
-            nc.scalar.copy(out=turned, in_=bank[:])
+        def turn_table(planes, name):
+            turned = keep.tile([P, TURNED, PACK, P], F32, name=name, align_bytes=64)
+            for j in range(TURNED):
+                bank = psum.tile([P, PACK, P], F32, name="turn_bank")
+                for t in range(PACK):
+                    nc.tensor.transpose(bank[:, t, :], planes[:, t, tokens(j)], ident[:])
+                nc.scalar.copy(out=turned[:, j, :, :], in_=bank[:])
+            return turned
 
-        def flat(ap):
-            return ap.rearrange("p a b -> p (a b)")
+        def multiply_plain(dst, bank, planes, j):
+            nc.vector.tensor_tensor(dst, bank[:], planes[:, :, tokens(j)], MULT)
 
-        def turn_sum(dst, left, right):
-            bank = psum.tile([P, PACK, TOK], F32, name="turn_bank")
-            for t in range(PACK):
-                nc.tensor.matmul(bank[:, t, :], left[:, t, :], ident[:], start=True, stop=False, is_transpose=True)
-                nc.tensor.matmul(bank[:, t, :], right[:, t, :], ident[:], start=False, stop=True, is_transpose=True)
-            nc.scalar.copy(out=dst.rearrange("p (c t) -> p c t", t=PACK), in_=bank[:].rearrange("p t c -> p c t"))
+        for t in range(1, PACK):
+            gather(c_planes, ct_planes, t)
+        c_turned = turn_table(c_planes, "c_turned")
+        gather(q_planes, st_planes, 0)
+        w1_bf = bf16_weight("w1")
+        w1_dealt, w1_read = dealt_views(w1_bf, w1_raw)
+        nc.scalar.copy(out=w1_dealt[:, :, :, 0:2], in_=w1_read[:, :, :, 0:2])
+        nc.vector.tensor_copy(out=w1_dealt[:, :, :, 2:4], in_=w1_read[:, :, :, 2:4])
+        gather(q_planes, st_planes, 1)
+        gather(q_planes, st_planes, 2)
+        w1_q = operand_tiles("w1", WIDTH)
+        for half in (1, 0):
+            words = slice(half * WIDTH // 2, (half + 1) * WIDTH // 2)
+            nc.vector.quantize_mx(
+                out=w1_q[0][:, words].bitcast(FP8X4),
+                scales=w1_q[1][:, words],
+                in_=w1_bf[:, words.start * PACK : words.stop * PACK],
+            )
 
-        def tile_of(name, j):
-            return keep.tile([P, PACK, TOK], F32, name=f"{name}{j}", align_bytes=64)
+        w2_bf = bf16_weight("w2")
+        w2_dealt, w2_read = dealt_views(w2_bf, w2_raw)
+        nc.scalar.copy(out=w2_dealt, in_=w2_read)
+        gather(q_planes, st_planes, 3)
+        q_turned = turn_table(q_planes, "q_turned")
+        w2_q = quantise(w2_bf[:], "w2")
 
-        y_plain, yc_plain = {}, {}
-        w3_bf = keep.tile([P, N * PACK], BF16, name="w3_bf", tag="w3_bf", align_bytes=64)
-        w4_bf = keep.tile([P, N * PACK], BF16, name="w4_bf", tag="w4_bf", align_bytes=64)
-        gather(c_planes, 1, ct1)
-        gather(c_planes, 2, ct2)
-        gather(c_planes, 3, ct3)
-        c_turned = keep.tile([P, TURNED, PACK, P], F32, name="c_turned", tag="c_turned", align_bytes=64)
-        for j in range(TURNED):
-            turn_table(c_turned[:, j, :, :], c_planes, j)
-        gather(q_planes, 0, st0)
-        w1_bf = group_first(w1_raw, "w1", True)
-        gather(q_planes, 1, st1)
-        gather(q_planes, 2, st2)
-        w1_q = quantise(w1_bf, "w1")
-        w2_bf = group_first(w2_raw, "w2", False)
-        gather(q_planes, 3, st3)
-        q_turned = keep.tile([P, TURNED, PACK, P], F32, name="q_turned", tag="q_turned", align_bytes=64)
-        for j in range(TURNED):
-            turn_table(q_turned[:, j, :, :], q_planes, j)
-        w2_q = quantise(w2_bf, "w2")
+        yc = keep.tile([P, TILES, PACK, TOK], F32, name="yc", tag="st2", align_bytes=64)
+        y_plain = {}
         for j in range(TURNED, TILES):
-            y_plain[j] = psum_one.tile([P, PACK, TOK], F32, name=f"y_plain{j}")
-            project(y_plain[j], w1_q, j)
-            yc_plain[j] = tile_of("yc", j)
-            product(yc_plain[j][:], y_plain[j], c_planes, j)
-        ec_turned = keep.tile([P, TURNED, PACK, P], F32, name="ec_turned", tag="ec_turned", align_bytes=64)
-        group_second(w3_bf, w3_raw, 0)
-        group_second(w3_bf, w3_raw, 1)
-        second = [quantise(w3_bf, "w3")]
-        group_second(w4_bf, w4_raw, 0)
+            y_plain[j] = psum_held.tile([P, PACK, TOK], F32, name=f"y_plain{j}")
+            project_plain(y_plain[j], w1_q, j)
+            multiply_plain(yc[:, j, :, :], y_plain[j], c_planes, j)
 
-        def rotate_turned(j):
+        last = TILES - 1
+        yq = keep.tile([P, last, PACK, TOK], F32, name="yq", tag="w2_bf", align_bytes=64)
+        for j in range(TURNED, last):
+            multiply_plain(yq[:, j, :, :], y_plain[j], q_planes, j)
+        for j in range(TURNED):
             y_bank = psum.tile([P, PACK, P], F32, name="y_bank")
-            e_bank = psum.tile([P, PACK, P], F32, name="e_bank")
             project_turned(y_bank, w1_q, j)
-            project_turned(e_bank, w2_q, j)
-            yc, minus_eq, yq = tile_of("yc", j), tile_of("minus_eq", j), tile_of("yq", j)
-            ec = ec_turned[:, j, :, :]
-            nc.vector.tensor_tensor(yc[:], y_bank[:], c_turned[:, j, :, :], MULT)
-            nc.vector.scalar_tensor_tensor(flat(minus_eq[:]), flat(e_bank[:]), -1.0, flat(q_turned[:, j, :, :]), MULT, MULT)
-            nc.vector.tensor_tensor(ec, e_bank[:], c_turned[:, j, :, :], MULT)
-            nc.vector.tensor_tensor(yq[:], y_bank[:], q_turned[:, j, :, :], MULT)
-            return yc[:], minus_eq[:], yq[:], ec
+            nc.vector.tensor_tensor(yc[:, j, :, :], y_bank[:], c_turned[:, j, :, :], MULT)
+            nc.vector.tensor_tensor(yq[:, j, :, :], y_bank[:], q_turned[:, j, :, :], MULT)
 
-        def sums_turned(j, parts):
-            z_bf = keep.tile([P, 2, TOK * PACK], BF16, name=f"z_bf{j}", tag=f"z_bf{j}", align_bytes=64)
-            turn_sum(z_bf[:, 0, :], parts[0], parts[1])
-            turn_sum(z_bf[:, 1, :], parts[2], parts[3])
+        w3_bf, w4_bf = bf16_weight("w3"), bf16_weight("w4")
+        round_half(w3_bf, w3_raw, 0)
+        round_half(w3_bf, w3_raw, 1)
+        w3_q = quantise(w3_bf[:], "w3")
+        round_half(w4_bf, w4_raw, 0)
+
+        def pairs_turned(j):
+            e_bank = psum.tile([P, PACK, P], F32, name="e_bank")
+            project_turned(e_bank, w2_q, j)
+            minus_eq, ec = product_tile(f"minus_eq{j}"), product_tile(f"ec{j}")
+            flat = "s t m -> s (t m)"
+            nc.vector.scalar_tensor_tensor(
+                minus_eq[:].rearrange(flat),
+                e_bank[:].rearrange(flat),
+                -1.0,
+                q_turned[:, j, :, :].rearrange(flat),
+                MULT,
+                MULT,
+            )
+            nc.vector.tensor_tensor(ec[:], e_bank[:], c_turned[:, j, :, :], MULT)
+            return (yc[:, j, :, :], minus_eq[:]), (yq[:, j, :, :], ec[:])
+
+        def z_tile(j):
+            return keep.tile([P, 2, TOK * PACK], BF16, name=f"z_bf{j}", align_bytes=64)
+
+        def sums_turned(j, pairs):
+            z_bf = z_tile(j)
+            for half, (left, right) in enumerate(pairs):
+                bank = psum.tile([P, PACK, TOK], F32, name="turn_bank")
+                for t in range(PACK):
+                    nc.tensor.matmul(bank[:, t, :], left[:, t, :], ident[:], start=True, stop=False, is_transpose=True)
+                    nc.tensor.matmul(bank[:, t, :], right[:, t, :], ident[:], start=False, stop=True, is_transpose=True)
+                nc.scalar.copy(
+                    out=z_bf[:, half, :].rearrange("p (s t) -> p s t", t=PACK),
+                    in_=bank[:].rearrange("p t s -> p s t"),
+                )
             return z_bf
 
-        def by_pairs(t):
-            return t.rearrange("p t (c i) -> p c t i", i=2)
-
-        def project_e(j):
+        def project_e_plain(j):
             e_bank = psum.tile([P, PACK, TOK], F32, name="e_bank")
-            project(e_bank, w2_q, j)
+            project_plain(e_bank, w2_q, j)
             return e_bank
 
-        def rotate_plain(j, e_bank, slot):
-            z_bf = keep.tile([P, 2, TOK * PACK], BF16, name=f"z_bf{j}", tag=f"z_bf{j}", align_bytes=64)
-            held = keep.tile([P, 3, PACK, TOK], F32, name=f"held{j}", tag=slot, align_bytes=64)
-            eq, ec, yq = held[:, 0, :, :], held[:, 1, :, :], held[:, 2, :, :]
-            product(eq, e_bank, q_planes, j)
-            product(ec, e_bank, c_planes, j)
-            product(yq, y_plain[j], q_planes, j)
-            woven = [z_bf[:, half, :].rearrange("p (c i t) -> p c t i", i=2, t=PACK) for half in range(2)]
-            nc.vector.tensor_tensor(woven[0], by_pairs(yc_plain[j][:]), by_pairs(eq), SUB)
-            nc.vector.tensor_tensor(woven[1], by_pairs(yq), by_pairs(ec), ADD)
+        def sum_plain(dst, left, right, op):
+            by_pairs = "p t (s i) -> p s t i"
+            nc.vector.tensor_tensor(
+                dst.rearrange("p (s i t) -> p s t i", i=2, t=PACK),
+                left.rearrange(by_pairs, i=2),
+                right.rearrange(by_pairs, i=2),
+                op,
+            )
+
+        def rotate_plain(j, e_bank):
+            z_bf = z_tile(j)
+            eq, ec = product_tile(f"eq{j}"), product_tile(f"ec{j}")
+            multiply_plain(eq[:], e_bank, q_planes, j)
+            multiply_plain(ec[:], e_bank, c_planes, j)
+            sum_plain(z_bf[:, 0, :], yc[:, j, :, :], eq[:], SUB)
+            sum_plain(z_bf[:, 1, :], yq[:, j, :, :], ec[:], ADD)
             return z_bf
 
-        def second_pass(dst, m, half, z_codes, z_scales, cols):
-            rows = slice(m * P, (m + 1) * P)
+        turned_pairs = [pairs_turned(j) for j in range(TURNED)]
+        e_plain = {j: project_e_plain(j) for j in range(TURNED, TILES)}
+        z_tiles = [sums_turned(0, turned_pairs[0])]
+        round_half(w4_bf, w4_raw, 1)
+        z_tiles.extend([sums_turned(j, turned_pairs[j]) for j in range(1, TURNED)])
+        z_tiles.extend([rotate_plain(j, e_plain[j]) for j in range(TURNED, last)])
+        w4_q = quantise(w4_bf[:], "w4")
+
+        def output_pass(dst, m, half, z_codes, z_scales):
+            codes, scales = (w3_q, w4_q)[half]
+            words = slice(m * P, (m + 1) * P)
             nc.tensor.matmul_mx(
                 out=dst,
-                lhsT=second[half][0][:, rows].bitcast(FP8X4),
-                lhsT_scale=second[half][1][:, rows],
-                rhs=z_codes[:, cols].bitcast(FP8X4),
-                rhs_scale=z_scales[:, cols],
+                lhsT=codes[:, words].bitcast(FP8X4),
+                lhsT_scale=scales[:, words],
+                rhs=z_codes.bitcast(FP8X4),
+                rhs_scale=z_scales,
                 start=(half == 0),
                 stop=(half == 1),
             )
 
-        out_tiles = out.rearrange("(m p) s -> p m s", p=P)
+        row_blocks = WIDTH // P
+        out_blocks = out.rearrange("(m p) s -> p m s", p=P)
 
         def finish(j, z_bf):
-            z_codes = keep.tile([P, 2 * TOK], U32, name=f"z_codes{j}", align_bytes=64)
-            z_scales = ring.tile([P, 2 * TOK], U8, name="z_scales", align_bytes=64)
-            nc.vector.quantize_mx(out=z_codes[:].bitcast(FP8X4), scales=z_scales[:], in_=z_bf[:].rearrange("p h n -> p (h n)"))
-            o_bank = psum.tile([P, PACK, TOK], F32, name="y_bank")
-            for m in range(N // P):
+            z_codes, z_scales = quantise(z_bf[:].rearrange("p h n -> p (h n)"), f"z{j}")
+            bank = psum.tile([P, row_blocks, TOK], F32, name="y_bank")
+            for m in range(row_blocks):
                 for half in range(2):
-                    second_pass(o_bank[:, m, :], m, half, z_codes, z_scales, slice(half * TOK, (half + 1) * TOK))
-            result = ring.tile([P, PACK, TOK], F32, name="result", align_bytes=64)
-            nc.scalar.copy(out=result[:], in_=o_bank[:])
-            nc.sync.dma_start(out_tiles[:, :, j * TOK : (j + 1) * TOK], result[:])
+                    output_pass(bank[:, m, :], m, half, z_codes[:, tokens(half)], z_scales[:, tokens(half)])
+            result = ring.tile([P, row_blocks, TOK], F32, name="result", align_bytes=64)
+            nc.scalar.copy(out=result[:], in_=bank[:])
+            nc.sync.dma_start(out_blocks[:, :, tokens(j)], result[:])
 
-        def rotate_and_finish_last(j, e_bank, slot):
-            z_bf = keep.tile([P, 2, TOK * PACK], BF16, name=f"z_bf{j}", align_bytes=64)
-            held = keep.tile([P, 3, PACK, TOK], F32, name=f"held{j}", tag=slot, align_bytes=64)
-            eq, ec, yq = held[:, 0, :, :], held[:, 1, :, :], held[:, 2, :, :]
-            woven = [z_bf[:, half, :].rearrange("p (c i t) -> p c t i", i=2, t=PACK) for half in range(2)]
-            banks = [psum.tile([P, TOK], F32, name=("turn_bank", "e_bank")[m // 2]) for m in range(N // P)]
+        for j in range(last):
+            finish(j, z_tiles[j])
 
-            def half_product(half):
-                z_codes = keep.tile([P, TOK], U32, name=f"last_codes{half}", align_bytes=64)
-                z_scales = keep.tile([P, TOK], U8, name=f"last_scales{half}", align_bytes=64)
-                nc.vector.quantize_mx(out=z_codes[:].bitcast(FP8X4), scales=z_scales[:], in_=z_bf[:, half, :])
-                for m in range(N // P):
-                    second_pass(banks[m][:], m, half, z_codes, z_scales, slice(0, TOK))
+        z_bf = z_tile(last)
+        late = keep.tile([P, 3, PACK, TOK], F32, name="late", tag="w4_bf", align_bytes=64)
+        eq_last, ec_last, yq_last = late[:, 0, :, :], late[:, 1, :, :], late[:, 2, :, :]
+        banks = [psum.tile([P, TOK], F32, name=("turn_bank", "e_bank")[m // 2]) for m in range(row_blocks)]
 
-            product(eq, e_bank, q_planes, j)
-            product(yq, y_plain[j], q_planes, j)
-            nc.vector.tensor_tensor(woven[0], by_pairs(yc_plain[j][:]), by_pairs(eq), SUB)
-            product(ec, e_bank, c_planes, j)
-            half_product(0)
-            nc.vector.tensor_tensor(woven[1], by_pairs(yq), by_pairs(ec), ADD)
-            half_product(1)
-            for pair, (copy, queue) in enumerate(((nc.scalar.copy, nc.scalar), (nc.vector.tensor_copy, nc.sync))):
-                result = keep.tile([P, 2, TOK], F32, name=f"last_result{pair}", align_bytes=64)
-                for m in range(2):
-                    copy(out=result[:, m, :], in_=banks[2 * pair + m][:])
-                queue.dma_start(out_tiles[:, 2 * pair : 2 * pair + 2, j * TOK : (j + 1) * TOK], result[:])
+        def last_passes(half):
+            z_codes, z_scales = quantise(z_bf[:, half, :], f"last{half}")
+            for m in range(row_blocks):
+                output_pass(banks[m][:], m, half, z_codes[:], z_scales[:])
 
-        p0 = rotate_turned(0)
-        p1 = rotate_turned(1)
-        e2 = project_e(2)
-        e3 = project_e(3)
-        z0 = sums_turned(0, p0)
-        group_second(w4_bf, w4_raw, 1)
-        z1 = sums_turned(1, p1)
-        z2 = rotate_plain(2, e2, "held2")
-        second.append(quantise(w4_bf, "w4"))
-        finish(0, z0)
-        finish(1, z1)
-        finish(2, z2)
-        rotate_and_finish_last(3, e3, "w4_bf")
+        multiply_plain(eq_last, e_plain[last], q_planes, last)
+        multiply_plain(yq_last, y_plain[last], q_planes, last)
+        sum_plain(z_bf[:, 0, :], yc[:, last, :, :], eq_last, SUB)
+        multiply_plain(ec_last, e_plain[last], c_planes, last)
+        last_passes(0)
+        sum_plain(z_bf[:, 1, :], yq_last, ec_last, ADD)
+        last_passes(1)
+        for pair, (copy, queue) in enumerate(((nc.scalar.copy, nc.scalar), (nc.vector.tensor_copy, nc.sync))):
+            result = keep.tile([P, 2, TOK], F32, name=f"last_result{pair}", align_bytes=64)
+            for m in range(2):
+                copy(out=result[:, m, :], in_=banks[2 * pair + m][:])
+            queue.dma_start(out_blocks[:, 2 * pair : 2 * pair + 2, tokens(last)], result[:])

@@ -198,7 +198,6 @@ def tile_picked_headrope_none_p_kernel(
         w3_bf, w4_bf = bf16_weight("w3"), bf16_weight("w4")
         round_half(w3_bf, w3_raw, 0)
         round_half(w3_bf, w3_raw, 1)
-        w3_q = quantise(w3_bf[:], "w3")
         round_half(w4_bf, w4_raw, 0)
 
         def pairs_turned(j):
@@ -223,7 +222,7 @@ def tile_picked_headrope_none_p_kernel(
         def sums_turned(j, pairs):
             z_bf = z_tile(j)
             for half, (left, right) in enumerate(pairs):
-                bank = psum.tile([P, PACK, TOK], F32, name="turn_bank")
+                bank = psum.tile([P, PACK, TOK], F32, name=("turn_bank", "y_bank")[j])
                 for t in range(PACK):
                     nc.tensor.matmul(bank[:, t, :], left[:, t, :], ident[:], start=True, stop=False, is_transpose=True)
                     nc.tensor.matmul(bank[:, t, :], right[:, t, :], ident[:], start=False, stop=True, is_transpose=True)
@@ -262,6 +261,7 @@ def tile_picked_headrope_none_p_kernel(
         round_half(w4_bf, w4_raw, 1)
         z_tiles.extend([sums_turned(j, turned_pairs[j]) for j in range(1, TURNED)])
         z_tiles.extend([rotate_plain(j, e_plain[j]) for j in range(TURNED, last)])
+        w3_q = quantise(w3_bf[:], "w3")
         w4_q = quantise(w4_bf[:], "w4")
 
         def output_pass(dst, m, half, z_codes, z_scales):
@@ -282,7 +282,7 @@ def tile_picked_headrope_none_p_kernel(
 
         def finish(j, z_bf):
             z_codes, z_scales = quantise(z_bf[:].rearrange("p h n -> p (h n)"), f"z{j}")
-            bank = psum.tile([P, row_blocks, TOK], F32, name="y_bank")
+            bank = psum.tile([P, row_blocks, TOK], F32, name="turn_bank")
             for m in range(row_blocks):
                 for half in range(2):
                     output_pass(bank[:, m, :], m, half, z_codes[:, tokens(half)], z_scales[:, tokens(half)])
@@ -290,13 +290,13 @@ def tile_picked_headrope_none_p_kernel(
             nc.scalar.copy(out=result[:], in_=bank[:])
             nc.sync.dma_start(out_blocks[:, :, tokens(j)], result[:])
 
-        for j in range(last):
-            finish(j, z_tiles[j])
+        finish(TURNED, z_tiles[TURNED])
+        finish(0, z_tiles[0])
 
         z_bf = z_tile(last)
         late = keep.tile([P, 3, PACK, TOK], F32, name="late", tag="w4_bf", align_bytes=64)
         eq_last, ec_last, yq_last = late[:, 0, :, :], late[:, 1, :, :], late[:, 2, :, :]
-        banks = [psum.tile([P, TOK], F32, name=("turn_bank", "e_bank")[m // 2]) for m in range(row_blocks)]
+        banks = [psum.tile([P, TOK], F32, name=("y_bank", "e_bank")[m // 2]) for m in range(row_blocks)]
 
         def last_passes(half):
             z_codes, z_scales = quantise(z_bf[:, half, :], f"last{half}")
@@ -305,6 +305,7 @@ def tile_picked_headrope_none_p_kernel(
 
         multiply_plain(eq_last, e_plain[last], q_planes, last)
         multiply_plain(yq_last, y_plain[last], q_planes, last)
+        finish(1, z_tiles[1])
         sum_plain(z_bf[:, 0, :], yc[:, last, :, :], eq_last, SUB)
         multiply_plain(ec_last, e_plain[last], c_planes, last)
         last_passes(0)

from contextlib import ExitStack

import concourse.mybir as mybir
from concourse.masks import make_identity

F32 = mybir.dt.float32
BF16 = mybir.dt.bfloat16
I32 = mybir.dt.int32
U32 = mybir.dt.uint32
U16 = mybir.dt.uint16
U8 = mybir.dt.uint8
FP8X4 = mybir.dt.float8_e4m3fn_x4
MULT = mybir.AluOpType.mult
ADD = mybir.AluOpType.add
SUB = mybir.AluOpType.subtract

P = 128
PACK = 4
TOKENS, PICKED, WIDTH, POSITIONS = 2048, 512, 512, 1024
TOK = 128
TILES = PICKED // TOK
TURNED = 2
FLOPS = 4 * 2 * 512 * 512 * 512


def tile_picked_headrope_none_p_kernel(
    tc, x_words, x_scales, w1, w2, ct, st, w3, w4, offs, pos, out
):
    nc = tc.nc
    with ExitStack() as ctx:
        keep = ctx.enter_context(tc.tile_pool(name="keep", bufs=1))
        ring = ctx.enter_context(tc.tile_pool(name="ring", bufs=TILES - 1))
        psum_held = ctx.enter_context(tc.psum_pool(name="psum_held", bufs=1))
        psum = ctx.enter_context(tc.psum_pool(name="psum", bufs=2))

        ident = keep.tile([P, P], F32, name="ident", align_bytes=64)
        make_identity(nc, ident[:])

        offs_sb = keep.tile([P, PICKED // 16], U16, name="offs_sb")
        pos_sb = keep.tile([P, PICKED // 16], U16, name="pos_sb")
        xs_all = keep.tile([P, TOKENS], U8, name="xs_all", align_bytes=64)
        nc.vector.memset(xs_all[:].bitcast(I32), 0)

        def load_plane(table, t, name):
            plane = keep.tile([P, POSITIONS], F32, name=f"{name}{t}", tag=f"{name}{t}", align_bytes=64)
            nc.sync.dma_start(plane[:], table.rearrange("(p t) u -> p t u", t=PACK)[:, t, :])
            return plane

        def load_weight(w, name):
            raw = keep.tile([P, PACK, WIDTH], F32, name=f"{name}_raw", align_bytes=64)
            nc.sync.dma_start(raw[:], w.rearrange("(p j) c -> p j c", j=PACK))
            return raw

        ct_planes = [load_plane(ct, 0, "ct")]
        nc.sync.dma_start(pos_sb[:], pos)
        nc.sync.dma_start(offs_sb[:], offs)
        for quad in range(4):
            nc.sync.dma_start(
                xs_all[32 * quad : 32 * quad + 4, :].bitcast(I32),
                x_scales[0, 4 * quad : 4 * quad + 4, :].bitcast(I32),
            )
        xw_all = keep.tile([P, TOKENS], U32, name="xw_all", align_bytes=64)
        nc.sync.dma_start(xw_all[:].bitcast(I32), x_words[0].rearrange("p n t -> p (n t)").bitcast(I32))
        ct_planes.extend([load_plane(ct, t, "ct") for t in (1, 2, 3)])
        st_planes = [load_plane(st, 0, "st")]
        w1_raw = load_weight(w1, "w1")
        st_planes.extend([load_plane(st, t, "st") for t in (1, 2)])
        w2_raw = load_weight(w2, "w2")
        st_planes.append(load_plane(st, 3, "st"))
        w3_raw = load_weight(w3, "w3")
        w4_raw = load_weight(w4, "w4")

        def operand_tiles(name, words):
            codes = keep.tile([P, words], U32, name=f"{name}_codes", align_bytes=64)
            scales = keep.tile([P, words], U8, name=f"{name}_scales", align_bytes=64)
            return codes, scales

        def quantise(grouped, name):
            codes, scales = operand_tiles(name, grouped.shape[1] // PACK)
            nc.vector.quantize_mx(out=codes[:].bitcast(FP8X4), scales=scales[:], in_=grouped)
            return codes, scales

        def bf16_weight(name):
            return keep.tile([P, WIDTH * PACK], BF16, name=f"{name}_bf", tag=f"{name}_bf", align_bytes=64)

        def dealt_views(grouped, raw):
            return (
                grouped[:].rearrange("p (t m j) -> p m j t", t=PACK, j=PACK),
                raw[:].rearrange("p j (m t) -> p m j t", t=PACK),
            )

        def round_half(grouped, raw, half):
            pairs = slice(half * WIDTH // 4, (half + 1) * WIDTH // 4)
            nc.scalar.copy(
                out=grouped[:].rearrange("p (c i j) -> p c j i", i=2, j=PACK)[:, pairs, :, :],
                in_=raw[:].rearrange("p j (c i) -> p c j i", i=2)[:, pairs, :, :],
            )

        c_planes = keep.tile([P, PACK, PICKED], F32, name="c_planes", align_bytes=64)
        q_planes = keep.tile([P, PACK, PICKED], F32, name="q_planes", align_bytes=64)

        def gather(planes, windows, t):
            nc.vector.tensor_copy(planes[:, t, :], windows[t][:].indirect(pos_sb[:]))

        def tokens(j):
            return slice(j * TOK, (j + 1) * TOK)

        def product_tile(name):
            return keep.tile([P, PACK, TOK], F32, name=name, align_bytes=64)

        xw = keep.tile([P, PICKED], U32, name="xw", align_bytes=64)
        gather(c_planes, ct_planes, 0)
        xs = keep.tile([P, PICKED], U8, name="xs", tag="ct0", align_bytes=64)
        nc.vector.tensor_copy(xs[:], xs_all[:].indirect(offs_sb[:]))
        nc.vector.tensor_copy(xw[:], xw_all[:].indirect(offs_sb[:]))

        def project_plain(bank, weight, j):
            codes, scales = weight
            for t in range(PACK):
                words = slice(t * P, (t + 1) * P)
                nc.tensor.matmul_mx(
                    out=bank[:, t, :],
                    lhsT=codes[:, words].bitcast(FP8X4),
                    lhsT_scale=scales[:, words],
                    rhs=xw[:, tokens(j)].bitcast(FP8X4),
                    rhs_scale=xs[:, tokens(j)],
                    start=True,
                    stop=True,
                )

        def project_turned(bank, weight, j):
            codes, scales = weight
            nc.tensor.matmul_mx(
                out=bank[:].rearrange("s t m -> s (t m)"),
                lhsT=xw[:, tokens(j)].bitcast(FP8X4),
                lhsT_scale=xs[:, tokens(j)],
                rhs=codes[:].bitcast(FP8X4),
                rhs_scale=scales[:],
                start=True,
                stop=True,
            )

        def turn_table(planes, name):
            turned = keep.tile([P, TURNED, PACK, P], F32, name=name, align_bytes=64)
            for j in range(TURNED):
                bank = psum.tile([P, PACK, P], F32, name="turn_bank")
                for t in range(PACK):
                    nc.tensor.transpose(bank[:, t, :], planes[:, t, tokens(j)], ident[:])
                nc.scalar.copy(out=turned[:, j, :, :], in_=bank[:])
            return turned

        def multiply_plain(dst, bank, planes, j):
            nc.vector.tensor_tensor(dst, bank[:], planes[:, :, tokens(j)], MULT)

        for t in range(1, PACK):
            gather(c_planes, ct_planes, t)
        c_turned = turn_table(c_planes, "c_turned")
        gather(q_planes, st_planes, 0)
        w1_bf = bf16_weight("w1")
        w1_dealt, w1_read = dealt_views(w1_bf, w1_raw)
        nc.scalar.copy(out=w1_dealt[:, :, :, 0:2], in_=w1_read[:, :, :, 0:2])
        nc.vector.tensor_copy(out=w1_dealt[:, :, :, 2:4], in_=w1_read[:, :, :, 2:4])
        gather(q_planes, st_planes, 1)
        gather(q_planes, st_planes, 2)
        w1_q = operand_tiles("w1", WIDTH)
        for half in (1, 0):
            words = slice(half * WIDTH // 2, (half + 1) * WIDTH // 2)
            nc.vector.quantize_mx(
                out=w1_q[0][:, words].bitcast(FP8X4),
                scales=w1_q[1][:, words],
                in_=w1_bf[:, words.start * PACK : words.stop * PACK],
            )

        w2_bf = bf16_weight("w2")
        w2_dealt, w2_read = dealt_views(w2_bf, w2_raw)
        nc.scalar.copy(out=w2_dealt, in_=w2_read)
        gather(q_planes, st_planes, 3)
        q_turned = turn_table(q_planes, "q_turned")
        w2_q = quantise(w2_bf[:], "w2")

        yc = keep.tile([P, TILES, PACK, TOK], F32, name="yc", tag="st2", align_bytes=64)
        y_plain = {}
        for j in range(TURNED, TILES):
            y_plain[j] = psum_held.tile([P, PACK, TOK], F32, name=f"y_plain{j}")
            project_plain(y_plain[j], w1_q, j)
            multiply_plain(yc[:, j, :, :], y_plain[j], c_planes, j)

        last = TILES - 1
        yq = keep.tile([P, last, PACK, TOK], F32, name="yq", tag="w2_bf", align_bytes=64)
        for j in range(TURNED, last):
            multiply_plain(yq[:, j, :, :], y_plain[j], q_planes, j)
        for j in range(TURNED):
            y_bank = psum.tile([P, PACK, P], F32, name="y_bank")
            project_turned(y_bank, w1_q, j)
            nc.vector.tensor_tensor(yc[:, j, :, :], y_bank[:], c_turned[:, j, :, :], MULT)
            nc.vector.tensor_tensor(yq[:, j, :, :], y_bank[:], q_turned[:, j, :, :], MULT)

        w3_bf, w4_bf = bf16_weight("w3"), bf16_weight("w4")
        round_half(w3_bf, w3_raw, 0)
        round_half(w3_bf, w3_raw, 1)
        round_half(w4_bf, w4_raw, 0)

        def pairs_turned(j):
            e_bank = psum.tile([P, PACK, P], F32, name="e_bank")
            project_turned(e_bank, w2_q, j)
            minus_eq, ec = product_tile(f"minus_eq{j}"), product_tile(f"ec{j}")
            flat = "s t m -> s (t m)"
            nc.vector.scalar_tensor_tensor(
                minus_eq[:].rearrange(flat),
                e_bank[:].rearrange(flat),
                -1.0,
                q_turned[:, j, :, :].rearrange(flat),
                MULT,
                MULT,
            )
            nc.vector.tensor_tensor(ec[:], e_bank[:], c_turned[:, j, :, :], MULT)
            return (yc[:, j, :, :], minus_eq[:]), (yq[:, j, :, :], ec[:])

        def z_tile(j):
            return keep.tile([P, 2, TOK * PACK], BF16, name=f"z_bf{j}", align_bytes=64)

        def sums_turned(j, pairs):
            z_bf = z_tile(j)
            for half, (left, right) in enumerate(pairs):
                bank = psum.tile([P, PACK, TOK], F32, name=("turn_bank", "y_bank")[j])
                for t in range(PACK):
                    nc.tensor.matmul(bank[:, t, :], left[:, t, :], ident[:], start=True, stop=False, is_transpose=True)
                    nc.tensor.matmul(bank[:, t, :], right[:, t, :], ident[:], start=False, stop=True, is_transpose=True)
                nc.scalar.copy(
                    out=z_bf[:, half, :].rearrange("p (s t) -> p s t", t=PACK),
                    in_=bank[:].rearrange("p t s -> p s t"),
                )
            return z_bf

        def project_e_plain(j):
            e_bank = psum.tile([P, PACK, TOK], F32, name="e_bank")
            project_plain(e_bank, w2_q, j)
            return e_bank

        def sum_plain(dst, left, right, op):
            by_pairs = "p t (s i) -> p s t i"
            nc.vector.tensor_tensor(
                dst.rearrange("p (s i t) -> p s t i", i=2, t=PACK),
                left.rearrange(by_pairs, i=2),
                right.rearrange(by_pairs, i=2),
                op,
            )

        def rotate_plain(j, e_bank):
            z_bf = z_tile(j)
            eq, ec = product_tile(f"eq{j}"), product_tile(f"ec{j}")
            multiply_plain(eq[:], e_bank, q_planes, j)
            multiply_plain(ec[:], e_bank, c_planes, j)
            sum_plain(z_bf[:, 0, :], yc[:, j, :, :], eq[:], SUB)
            sum_plain(z_bf[:, 1, :], yq[:, j, :, :], ec[:], ADD)
            return z_bf

        turned_pairs = [pairs_turned(j) for j in range(TURNED)]
        e_plain = {j: project_e_plain(j) for j in range(TURNED, TILES)}
        z_tiles = [sums_turned(0, turned_pairs[0])]
        round_half(w4_bf, w4_raw, 1)
        z_tiles.extend([sums_turned(j, turned_pairs[j]) for j in range(1, TURNED)])
        z_tiles.extend([rotate_plain(j, e_plain[j]) for j in range(TURNED, last)])
        w3_q = quantise(w3_bf[:], "w3")
        w4_q = quantise(w4_bf[:], "w4")

        def output_pass(dst, m, half, z_codes, z_scales):
            codes, scales = (w3_q, w4_q)[half]
            words = slice(m * P, (m + 1) * P)
            nc.tensor.matmul_mx(
                out=dst,
                lhsT=codes[:, words].bitcast(FP8X4),
                lhsT_scale=scales[:, words],
                rhs=z_codes.bitcast(FP8X4),
                rhs_scale=z_scales,
                start=(half == 0),
                stop=(half == 1),
            )

        row_blocks = WIDTH // P
        out_blocks = out.rearrange("(m p) s -> p m s", p=P)

        def finish(j, z_bf):
            z_codes, z_scales = quantise(z_bf[:].rearrange("p h n -> p (h n)"), f"z{j}")
            bank = psum.tile([P, row_blocks, TOK], F32, name="turn_bank")
            for m in range(row_blocks):
                for half in range(2):
                    output_pass(bank[:, m, :], m, half, z_codes[:, tokens(half)], z_scales[:, tokens(half)])
            result = ring.tile([P, row_blocks, TOK], F32, name="result", align_bytes=64)
            nc.scalar.copy(out=result[:], in_=bank[:])
            nc.sync.dma_start(out_blocks[:, :, tokens(j)], result[:])

        finish(TURNED, z_tiles[TURNED])
        finish(0, z_tiles[0])

        z_bf = z_tile(last)
        late = keep.tile([P, 3, PACK, TOK], F32, name="late", tag="w4_bf", align_bytes=64)
        eq_last, ec_last, yq_last = late[:, 0, :, :], late[:, 1, :, :], late[:, 2, :, :]
        banks = [psum.tile([P, TOK], F32, name=("y_bank", "e_bank")[m // 2]) for m in range(row_blocks)]

        def last_passes(half):
            z_codes, z_scales = quantise(z_bf[:, half, :], f"last{half}")
            for m in range(row_blocks):
                output_pass(banks[m][:], m, half, z_codes[:], z_scales[:])

        multiply_plain(eq_last, e_plain[last], q_planes, last)
        multiply_plain(yq_last, y_plain[last], q_planes, last)
        finish(1, z_tiles[1])
        sum_plain(z_bf[:, 0, :], yc[:, last, :, :], eq_last, SUB)
        multiply_plain(ec_last, e_plain[last], c_planes, last)
        last_passes(0)
        sum_plain(z_bf[:, 1, :], yq_last, ec_last, ADD)
        last_passes(1)
        for pair, (copy, queue) in enumerate(((nc.scalar.copy, nc.scalar), (nc.vector.tensor_copy, nc.sync))):
            result = keep.tile([P, 2, TOK], F32, name=f"last_result{pair}", align_bytes=64)
            for m in range(2):
                copy(out=result[:, m, :], in_=banks[2 * pair + m][:])
            queue.dma_start(out_blocks[:, 2 * pair : 2 * pair + 2, tokens(last)], result[:])
